import numpy as np, ml_dtypes
CORES = [4,20,36,52,68,84,100,116,132,148,164,180,196,212,228,244]
N = 16
TK, LAY = 256, 4
def setup_inputs(rng):
    return {"x": rng.standard_normal((N, 128, TK), dtype=np.float32).astype(ml_dtypes.bfloat16), "w": (rng.standard_normal((N, 128, LAY * 256), dtype=np.float32) / 16).astype(ml_dtypes.bfloat16)}
def setup_inputs_big(rng):
    d = setup_inputs(rng)
    for k in ("x", "w"): d[k] = (d[k].astype(np.float32) * 1024.0).astype(d[k].dtype)
    return d
def setup_inputs_small(rng):
    d = setup_inputs(rng)
    for k in ("x", "w"): d[k] = (d[k].astype(np.float32) * (1 / 1024.0)).astype(d[k].dtype)
    return d
def setup_inputs_apart(rng):
    d = setup_inputs(rng)
    f = (10.0 ** rng.permutation(np.linspace(-1.5, 1.5, N))).astype(np.float32).reshape(N, 1, 1)
    for k in ("x", "w"): d[k] = (d[k].astype(np.float32) * f).astype(d[k].dtype)
    return d
def reference(x, w):
    X, W = x.astype(np.float64), w.astype(np.float64)
    h = list(X)
    for l in range(LAY):
        h = [np.maximum(W[r][:, 256 * l:256 * l + 128].T @ h[r] + W[r][:, 256 * l + 128:256 * l + 256].T @ h[r ^ (1 << l)], 0.0) for r in range(N)]
    return {"y": np.stack(h).astype(ml_dtypes.bfloat16)}

@@ -1,0 +1,166 @@
+from concourse.bass import DstId, RemoteDMATransfer
+from concourse.mybir import AluOpType
+
+P, TK, LAY = 128, 256, 4
+NCH = 2
+CW = TK // NCH
+PLAN = (("one", 0), ("one", 1), ("two", 2))
+NSTAGE = sum(1 if kind == "one" else 3 for kind, _ in PLAN)
+
+SCRATCH = {
+    "ws": ("sbuf", [P, LAY * 256], "bfloat16"),
+    "zero": ("sbuf", [P, CW], "bfloat16"),
+}
+for _i in range(LAY + 1):
+    SCRATCH["h%d" % _i] = ("sbuf", [P, TK], "bfloat16")
+for _i in range(8):
+    SCRATCH["acc%d" % _i] = ("psum", [P, 512], "float32")
+SEMAPHORES = ["sx", "sw0", "sw", "sz", "sy", "sent"]
+for _kind, _l in PLAN:
+    SEMAPHORES.append("ar%d" % _l)
+    if _kind == "one":
+        SCRATCH["p%d" % _l] = ("sbuf", [P, TK], "bfloat16")
+    else:
+        for _n in ("qa", "qb", "qc", "wq", "gm"):
+            SCRATCH["%s%d" % (_n, _l)] = ("sbuf", [P, TK], "bfloat16")
+        SEMAPHORES.append("aw%d" % _l)
+for _i in range(NSTAGE):
+    for _c in range(NCH):
+        SEMAPHORES += ["m%d_%d" % (_i, _c), "v%d_%d" % (_i, _c)]
+
+
+def rank_program(g, core, T, topo):
+    rank = T.rank_of(core)
+    if rank is None:
+        return
+    S = T.sem
+    te, ve = g.tensor, g.vector
+    cols = [slice(c * CW, (c + 1) * CW) for c in range(NCH)]
+    count = {"bank": 0, "stage": 0, "sent": 0}
+    waited = set()
+
+    def u(l):
+        return T.ws[:, 256 * l:256 * l + 128]
+
+    def v(l):
+        return T.ws[:, 256 * l + 128:256 * l + 256]
+
+    def send(src, dests, sem):
+        mask, ids = None, []
+        for q, _ in dests:
+            d = T.cores[q]
+            assert topo.may_write(core, d)
+            m = topo.mask(core, d)
+            mask = m if mask is None else (mask & m)
+            rid, pid = topo.addr(d, core)
+            ids.append((rid, pid))
+        n = bin(mask).count("1")
+        if len(dests) == 1:
+            g.remote_dma(out_ap=dests[0][1][:], in_ap=src, remote_sem=sem, local_sem=S.sent,
+                         pid=ids[0][1], routing_id=ids[0][0], dma_engine_mask=mask)
+        else:
+            g.remote_dma_fused([RemoteDMATransfer(dst_ids=[DstId(rid=a, pnc=b) for a, b in ids], dma_engine_mask=mask,
+                                                  remote_sem=sem, srcs=[src], dsts=[b[:] for _, b in dests], alu_op=0)],
+                               local_sem=S.sent)
+        count["sent"] += n
+        return n
+
+    def new_stage():
+        s = count["stage"]
+        count["stage"] += 1
+        acc = []
+        for c in range(NCH):
+            acc.append(T["acc%d" % (count["bank"] % 8)][:, 0:CW])
+            count["bank"] += 1
+        return {"acc": acc, "m": ["m%d_%d" % (s, c) for c in range(NCH)], "v": ["v%d_%d" % (s, c) for c in range(NCH)]}
+
+    def mm(st, c, lhsT, rhs, start, stop):
+        ins = te.matmul(out=st["acc"][c], lhsT=lhsT, rhs=rhs[:, cols[c]], start=start, stop=stop)
+        if stop:
+            ins.then_inc(S[st["m"][c]], 1)
+
+    def relu(st, out):
+        for c in range(NCH):
+            ve.wait_ge(S[st["m"][c]], 1)
+            ve.tensor_tensor(out=out[:, cols[c]], in0=st["acc"][c], in1=T.zero[:], op=AluOpType.max).then_inc(S[st["v"][c]], 1)
+        return [(st["v"][c], 1) for c in range(NCH)]
+
+    def wait_all(q, ready):
+        seen = []
+        for name, val in reversed(ready):
+            if name not in seen:
+                seen.append(name)
+                q.wait_ge(S[name], val)
+
+    def te_wait_w(l):
+        name = "sw0" if l == 0 else "sw"
+        if name not in waited:
+            waited.add(name)
+            te.wait_ge(S[name], 16)
+
+    g.sync.dma_start(out=T.h0[:], in_=T.x[:]).then_inc(S.sx, 16)
+    w0_queue = g.scalar if PLAN[0][0] == "two" else g.sync
+    w0_queue.dma_start(out=T.ws[:, 0:256], in_=T.w[:, 0:256]).then_inc(S.sw0, 16)
+    g.sync.dma_start(out=T.ws[:, 256:], in_=T.w[:, 256:]).then_inc(S.sw, 16)
+    ve.memset(T.zero[:], 0.0).then_inc(S.sz, 1)
+    ve.wait_ge(S.sz, 1)
+
+    w_sent = set()
+
+    def send_weights(l):
+        if l in w_sent:
+            return
+        w_sent.add(l)
+        g.wait_ge(S.sw0 if l == 0 else S.sw, 16)
+        send(T.ws[:, 256 * l:256 * l + 256], [(rank ^ (2 << l), T["wq%d" % l])], S["aw%d" % l])
+
+    ready = [("sx", 16)] * NCH
+    for i, (kind, l) in enumerate(PLAN):
+        hin = T["h%d" % l]
+        a, b = 1 << l, 2 << l
+        wait_all(g, ready)
+        if kind == "one":
+            n_arr = send(hin[:], [(rank ^ a, T["p%d" % l])], S["ar%d" % l])
+        else:
+            n_arr = 3 * send(hin[:], [(rank ^ a, T["qa%d" % l]), (rank ^ b, T["qb%d" % l]), (rank ^ a ^ b, T["qc%d" % l])],
+                             S["ar%d" % l])
+            send_weights(l)
+        if i + 1 < len(PLAN) and PLAN[i + 1][0] == "two":
+            send_weights(PLAN[i + 1][1])
+
+        te_wait_w(l)
+        st = new_stage()
+        for c in range(NCH):
+            if c == 0 or ready[c] != ready[c - 1]:
+                te.wait_ge(S[ready[c][0]], ready[c][1])
+            mm(st, c, u(l), hin, True, False)
+        te.wait_ge(S["ar%d" % l], n_arr)
+        if kind == "one":
+            for c in range(NCH):
+                mm(st, c, v(l), T["p%d" % l], False, True)
+            ready = relu(st, T["h%d" % (l + 1)])
+            continue
+        for c in range(NCH):
+            mm(st, c, v(l), T["qa%d" % l], False, True)
+        mid = relu(st, T["h%d" % (l + 1)])
+        te.wait_ge(S["aw%d" % l], n_arr // 3)
+        sb = new_stage()
+        wq = T["wq%d" % l]
+        for c in range(NCH):
+            mm(sb, c, wq[:, 0:128], T["qb%d" % l], True, False)
+            mm(sb, c, wq[:, 128:256], T["qc%d" % l], False, True)
+        gmid = relu(sb, T["gm%d" % l])
+        te_wait_w(l + 1)
+        sc = new_stage()
+        for c in range(NCH):
+            te.wait_ge(S[mid[c][0]], mid[c][1])
+            mm(sc, c, u(l + 1), T["h%d" % (l + 1)], True, False)
+        for c in range(NCH):
+            te.wait_ge(S[gmid[c][0]], gmid[c][1])
+            mm(sc, c, v(l + 1), T["gm%d" % l], False, True)
+        ready = relu(sc, T["h%d" % (l + 2)])
+
+    wait_all(g.sync, ready)
+    g.sync.dma_start(out=T.y[:], in_=T["h%d" % LAY][:]).then_inc(S.sy, 16)
+    g.sync.wait_ge(S.sy, 16)
+    g.wait_ge(S.sent, count["sent"])

@@ -2,31 +2,27 @@ from concourse.bass import DstId, RemoteDMATransfer
 from concourse.mybir import AluOpType
 
 P, TK, LAY = 128, 256, 4
-NCH = 2
+NCH = 4
 CW = TK // NCH
-PLAN = (("one", 0), ("one", 1), ("two", 2))
-NSTAGE = sum(1 if kind == "one" else 3 for kind, _ in PLAN)
+NST = 2
+STAGES = ("s0", "s1", "sa", "sg", "sb", "sc")
 
 SCRATCH = {
     "ws": ("sbuf", [P, LAY * 256], "bfloat16"),
+    "wq": ("sbuf", [P, 512], "bfloat16"),
     "zero": ("sbuf", [P, CW], "bfloat16"),
 }
-for _i in range(LAY + 1):
-    SCRATCH["h%d" % _i] = ("sbuf", [P, TK], "bfloat16")
-for _i in range(8):
+for _n in ("h0", "h1", "h2", "h3", "h4",
+           "p0", "p1",
+           "ea", "eb", "k2",
+           "qa", "qc", "gm"):
+    SCRATCH[_n] = ("sbuf", [P, TK], "bfloat16")
+for _i in range(2 * NCH):
     SCRATCH["acc%d" % _i] = ("psum", [P, 512], "float32")
-SEMAPHORES = ["sx", "sw0", "sw", "sz", "sy", "sent"]
-for _kind, _l in PLAN:
-    SEMAPHORES.append("ar%d" % _l)
-    if _kind == "one":
-        SCRATCH["p%d" % _l] = ("sbuf", [P, TK], "bfloat16")
-    else:
-        for _n in ("qa", "qb", "qc", "wq", "gm"):
-            SCRATCH["%s%d" % (_n, _l)] = ("sbuf", [P, TK], "bfloat16")
-        SEMAPHORES.append("aw%d" % _l)
-for _i in range(NSTAGE):
+SEMAPHORES = ["sx", "sw0", "sw12", "sw3", "sz", "sent", "ar0", "ar1", "ae", "aw", "aqc", "aqa"] + ["sy%d" % _k for _k in range(NST)]
+for _n in STAGES:
     for _c in range(NCH):
-        SEMAPHORES += ["m%d_%d" % (_i, _c), "v%d_%d" % (_i, _c)]
+        SEMAPHORES += ["m%s_%d" % (_n, _c), "v%s_%d" % (_n, _c)]
 
 
 def rank_program(g, core, T, topo):
@@ -35,9 +31,9 @@ def rank_program(g, core, T, topo):
         return
     S = T.sem
     te, ve = g.tensor, g.vector
-    cols = [slice(c * CW, (c + 1) * CW) for c in range(NCH)]
-    count = {"bank": 0, "stage": 0, "sent": 0}
-    waited = set()
+    CH = range(NCH)
+    cols = [slice(c * CW, (c + 1) * CW) for c in CH]
+    count = {"sent": 0}
 
     def u(l):
         return T.ws[:, 256 * l:256 * l + 128]
@@ -65,102 +61,90 @@ def rank_program(g, core, T, topo):
         count["sent"] += n
         return n
 
-    def new_stage():
-        s = count["stage"]
-        count["stage"] += 1
-        acc = []
-        for c in range(NCH):
-            acc.append(T["acc%d" % (count["bank"] % 8)][:, 0:CW])
-            count["bank"] += 1
-        return {"acc": acc, "m": ["m%d_%d" % (s, c) for c in range(NCH)], "v": ["v%d_%d" % (s, c) for c in range(NCH)]}
-
-    def mm(st, c, lhsT, rhs, start, stop):
-        ins = te.matmul(out=st["acc"][c], lhsT=lhsT, rhs=rhs[:, cols[c]], start=start, stop=stop)
+    def mm(st, bank_set, c, lhsT, rhs, start, stop):
+        ins = te.matmul(out=T["acc%d" % (NCH * bank_set + c)][:, 0:CW], lhsT=lhsT, rhs=rhs[:, cols[c]], start=start, stop=stop)
         if stop:
-            ins.then_inc(S[st["m"][c]], 1)
+            ins.then_inc(S["m%s_%d" % (st, c)], 1)
 
-    def relu(st, out):
-        for c in range(NCH):
-            ve.wait_ge(S[st["m"][c]], 1)
-            ve.tensor_tensor(out=out[:, cols[c]], in0=st["acc"][c], in1=T.zero[:], op=AluOpType.max).then_inc(S[st["v"][c]], 1)
-        return [(st["v"][c], 1) for c in range(NCH)]
+    def relu(st, bank_set, c, out):
+        ve.wait_ge(S["m%s_%d" % (st, c)], 1)
+        ve.tensor_tensor(out=out[:, cols[c]], in0=T["acc%d" % (NCH * bank_set + c)][:, 0:CW], in1=T.zero[:],
+                         op=AluOpType.max).then_inc(S["v%s_%d" % (st, c)], 1)
 
-    def wait_all(q, ready):
-        seen = []
-        for name, val in reversed(ready):
-            if name not in seen:
-                seen.append(name)
-                q.wait_ge(S[name], val)
+    def done(q, st, c):
+        q.wait_ge(S["v%s_%d" % (st, c)], 1)
 
-    def te_wait_w(l):
-        name = "sw0" if l == 0 else "sw"
-        if name not in waited:
-            waited.add(name)
-            te.wait_ge(S[name], 16)
+    def all_done(q, st, blocks):
+        for c in reversed(blocks):
+            done(q, st, c)
 
     g.sync.dma_start(out=T.h0[:], in_=T.x[:]).then_inc(S.sx, 16)
-    w0_queue = g.scalar if PLAN[0][0] == "two" else g.sync
-    w0_queue.dma_start(out=T.ws[:, 0:256], in_=T.w[:, 0:256]).then_inc(S.sw0, 16)
-    g.sync.dma_start(out=T.ws[:, 256:], in_=T.w[:, 256:]).then_inc(S.sw, 16)
+    g.sync.dma_start(out=T.ws[:, 256:768], in_=T.w[:, 256:768]).then_inc(S.sw12, 16)
+    g.sync.dma_start(out=T.ws[:, 0:256], in_=T.w[:, 0:256]).then_inc(S.sw0, 16)
+    g.sync.dma_start(out=T.ws[:, 768:1024], in_=T.w[:, 768:1024]).then_inc(S.sw3, 16)
     ve.memset(T.zero[:], 0.0).then_inc(S.sz, 1)
     ve.wait_ge(S.sz, 1)
 
-    w_sent = set()
+    g.wait_ge(S.sx, 16)
+    n = send(T.h0[:], [(rank ^ 1, T.p0)], S.ar0)
+    g.wait_ge(S.sw12, 16)
+    send(T.ws[:, 256:768], [(rank ^ 8, T.wq)], S.aw)
+    all_done(g, "s0", list(CH))
+    send(T.h1[:], [(rank ^ 2, T.p1)], S.ar1)
+    send(T.h1[:], [(rank ^ 8, T.ea), (rank ^ 10, T.eb)], S.ae)
+    all_done(g, "s1", list(CH))
+    send(T.h2[:], [(rank ^ 12, T.qc)], S.aqc)
+    send(T.h2[:], [(rank ^ 4, T.qa)], S.aqa)
 
-    def send_weights(l):
-        if l in w_sent:
-            return
-        w_sent.add(l)
-        g.wait_ge(S.sw0 if l == 0 else S.sw, 16)
-        send(T.ws[:, 256 * l:256 * l + 256], [(rank ^ (2 << l), T["wq%d" % l])], S["aw%d" % l])
+    te.wait_ge(S.sx, 16)
+    te.wait_ge(S.sw0, 16)
+    for c in CH:
+        mm("s0", 1, c, u(0), T.h0, True, False)
+    te.wait_ge(S.ar0, n)
+    for c in CH:
+        mm("s0", 1, c, v(0), T.p0, False, True)
+        relu("s0", 1, c, T.h1)
+    te.wait_ge(S.sw12, 16)
+    for c in CH:
+        done(te, "s0", c)
+        mm("s1", 0, c, u(1), T.h1, True, False)
+    te.wait_ge(S.ar1, n)
+    for c in CH:
+        mm("s1", 0, c, v(1), T.p1, False, True)
+        relu("s1", 0, c, T.h2)
+    for c in CH:
+        done(te, "s1", c)
+        mm("sa", 1, c, u(2), T.h2, True, False)
+    te.wait_ge(S.aw, n)
+    te.wait_ge(S.ae, 2 * n)
+    for c in CH:
+        mm("sg", 0, c, T.wq[:, 0:128], T.ea, True, False)
+        mm("sg", 0, c, T.wq[:, 128:256], T.eb, False, True)
+        relu("sg", 0, c, T.k2)
+    for c in CH:
+        done(te, "sg", c)
+        mm("sb", 0, c, T.wq[:, 256:384], T.k2, True, False)
+    te.wait_ge(S.aqc, n)
+    for c in CH:
+        mm("sb", 0, c, T.wq[:, 384:512], T.qc, False, True)
+        relu("sb", 0, c, T.gm)
+    te.wait_ge(S.aqa, n)
+    for c in CH:
+        mm("sa", 1, c, v(2), T.qa, False, True)
+        relu("sa", 1, c, T.h3)
+    te.wait_ge(S.sw3, 16)
+    for c in CH:
+        done(te, "sb", c)
+        mm("sc", 0, c, v(3), T.gm, True, False)
+        done(te, "sa", c)
+        mm("sc", 0, c, u(3), T.h3, False, True)
+        relu("sc", 0, c, T.h4)
 
-    ready = [("sx", 16)] * NCH
-    for i, (kind, l) in enumerate(PLAN):
-        hin = T["h%d" % l]
-        a, b = 1 << l, 2 << l
-        wait_all(g, ready)
-        if kind == "one":
-            n_arr = send(hin[:], [(rank ^ a, T["p%d" % l])], S["ar%d" % l])
-        else:
-            n_arr = 3 * send(hin[:], [(rank ^ a, T["qa%d" % l]), (rank ^ b, T["qb%d" % l]), (rank ^ a ^ b, T["qc%d" % l])],
-                             S["ar%d" % l])
-            send_weights(l)
-        if i + 1 < len(PLAN) and PLAN[i + 1][0] == "two":
-            send_weights(PLAN[i + 1][1])
-
-        te_wait_w(l)
-        st = new_stage()
-        for c in range(NCH):
-            if c == 0 or ready[c] != ready[c - 1]:
-                te.wait_ge(S[ready[c][0]], ready[c][1])
-            mm(st, c, u(l), hin, True, False)
-        te.wait_ge(S["ar%d" % l], n_arr)
-        if kind == "one":
-            for c in range(NCH):
-                mm(st, c, v(l), T["p%d" % l], False, True)
-            ready = relu(st, T["h%d" % (l + 1)])
-            continue
-        for c in range(NCH):
-            mm(st, c, v(l), T["qa%d" % l], False, True)
-        mid = relu(st, T["h%d" % (l + 1)])
-        te.wait_ge(S["aw%d" % l], n_arr // 3)
-        sb = new_stage()
-        wq = T["wq%d" % l]
-        for c in range(NCH):
-            mm(sb, c, wq[:, 0:128], T["qb%d" % l], True, False)
-            mm(sb, c, wq[:, 128:256], T["qc%d" % l], False, True)
-        gmid = relu(sb, T["gm%d" % l])
-        te_wait_w(l + 1)
-        sc = new_stage()
-        for c in range(NCH):
-            te.wait_ge(S[mid[c][0]], mid[c][1])
-            mm(sc, c, u(l + 1), T["h%d" % (l + 1)], True, False)
-        for c in range(NCH):
-            te.wait_ge(S[gmid[c][0]], gmid[c][1])
-            mm(sc, c, v(l + 1), T["gm%d" % l], False, True)
-        ready = relu(sc, T["h%d" % (l + 2)])
-
-    wait_all(g.sync, ready)
-    g.sync.dma_start(out=T.y[:], in_=T["h%d" % LAY][:]).then_inc(S.sy, 16)
-    g.sync.wait_ge(S.sy, 16)
+    per = NCH // NST
+    for k in range(NST):
+        q = g.sync if k == NST - 1 else g.scalar
+        all_done(q, "sc", list(range(k * per, (k + 1) * per)))
+        piece = slice(k * per * CW, (k + 1) * per * CW)
+        q.dma_start(out=T.y[:, piece], in_=T.h4[:, piece]).then_inc(S["sy%d" % k], 16)
+        q.wait_ge(S["sy%d" % k], 16)
     g.wait_ge(S.sent, count["sent"])

from concourse.bass import DstId, RemoteDMATransfer
from concourse.mybir import AluOpType

P, TK, LAY = 128, 256, 4
NCH = 4
CW = TK // NCH
NST = 2
STAGES = ("s0", "s1", "sa", "sg", "sb", "sc")

SCRATCH = {
    "ws": ("sbuf", [P, LAY * 256], "bfloat16"),
    "wq": ("sbuf", [P, 512], "bfloat16"),
    "zero": ("sbuf", [P, CW], "bfloat16"),
}
for _n in ("h0", "h1", "h2", "h3", "h4",
           "p0", "p1",
           "ea", "eb", "k2",
           "qa", "qc", "gm"):
    SCRATCH[_n] = ("sbuf", [P, TK], "bfloat16")
for _i in range(2 * NCH):
    SCRATCH["acc%d" % _i] = ("psum", [P, 512], "float32")
SEMAPHORES = ["sx", "sw0", "sw12", "sw3", "sz", "sent", "ar0", "ar1", "ae", "aw", "aqc", "aqa"] + ["sy%d" % _k for _k in range(NST)]
for _n in STAGES:
    for _c in range(NCH):
        SEMAPHORES += ["m%s_%d" % (_n, _c), "v%s_%d" % (_n, _c)]


def rank_program(g, core, T, topo):
    rank = T.rank_of(core)
    if rank is None:
        return
    S = T.sem
    te, ve = g.tensor, g.vector
    CH = range(NCH)
    cols = [slice(c * CW, (c + 1) * CW) for c in CH]
    count = {"sent": 0}

    def u(l):
        return T.ws[:, 256 * l:256 * l + 128]

    def v(l):
        return T.ws[:, 256 * l + 128:256 * l + 256]

    def send(src, dests, sem):
        mask, ids = None, []
        for q, _ in dests:
            d = T.cores[q]
            assert topo.may_write(core, d)
            m = topo.mask(core, d)
            mask = m if mask is None else (mask & m)
            rid, pid = topo.addr(d, core)
            ids.append((rid, pid))
        n = bin(mask).count("1")
        if len(dests) == 1:
            g.remote_dma(out_ap=dests[0][1][:], in_ap=src, remote_sem=sem, local_sem=S.sent,
                         pid=ids[0][1], routing_id=ids[0][0], dma_engine_mask=mask)
        else:
            g.remote_dma_fused([RemoteDMATransfer(dst_ids=[DstId(rid=a, pnc=b) for a, b in ids], dma_engine_mask=mask,
                                                  remote_sem=sem, srcs=[src], dsts=[b[:] for _, b in dests], alu_op=0)],
                               local_sem=S.sent)
        count["sent"] += n
        return n

    def mm(st, bank_set, c, lhsT, rhs, start, stop):
        ins = te.matmul(out=T["acc%d" % (NCH * bank_set + c)][:, 0:CW], lhsT=lhsT, rhs=rhs[:, cols[c]], start=start, stop=stop)
        if stop:
            ins.then_inc(S["m%s_%d" % (st, c)], 1)

    def relu(st, bank_set, c, out):
        ve.wait_ge(S["m%s_%d" % (st, c)], 1)
        ve.tensor_tensor(out=out[:, cols[c]], in0=T["acc%d" % (NCH * bank_set + c)][:, 0:CW], in1=T.zero[:],
                         op=AluOpType.max).then_inc(S["v%s_%d" % (st, c)], 1)

    def done(q, st, c):
        q.wait_ge(S["v%s_%d" % (st, c)], 1)

    def all_done(q, st, blocks):
        for c in reversed(blocks):
            done(q, st, c)

    g.sync.dma_start(out=T.h0[:], in_=T.x[:]).then_inc(S.sx, 16)
    g.sync.dma_start(out=T.ws[:, 256:768], in_=T.w[:, 256:768]).then_inc(S.sw12, 16)
    g.sync.dma_start(out=T.ws[:, 0:256], in_=T.w[:, 0:256]).then_inc(S.sw0, 16)
    g.sync.dma_start(out=T.ws[:, 768:1024], in_=T.w[:, 768:1024]).then_inc(S.sw3, 16)
    ve.memset(T.zero[:], 0.0).then_inc(S.sz, 1)
    ve.wait_ge(S.sz, 1)

    g.wait_ge(S.sx, 16)
    n = send(T.h0[:], [(rank ^ 1, T.p0)], S.ar0)
    g.wait_ge(S.sw12, 16)
    send(T.ws[:, 256:768], [(rank ^ 8, T.wq)], S.aw)
    all_done(g, "s0", list(CH))
    send(T.h1[:], [(rank ^ 2, T.p1)], S.ar1)
    send(T.h1[:], [(rank ^ 8, T.ea), (rank ^ 10, T.eb)], S.ae)
    all_done(g, "s1", list(CH))
    send(T.h2[:], [(rank ^ 12, T.qc)], S.aqc)
    send(T.h2[:], [(rank ^ 4, T.qa)], S.aqa)

    te.wait_ge(S.sx, 16)
    te.wait_ge(S.sw0, 16)
    for c in CH:
        mm("s0", 1, c, u(0), T.h0, True, False)
    te.wait_ge(S.ar0, n)
    for c in CH:
        mm("s0", 1, c, v(0), T.p0, False, True)
        relu("s0", 1, c, T.h1)
    te.wait_ge(S.sw12, 16)
    for c in CH:
        done(te, "s0", c)
        mm("s1", 0, c, u(1), T.h1, True, False)
    te.wait_ge(S.ar1, n)
    for c in CH:
        mm("s1", 0, c, v(1), T.p1, False, True)
        relu("s1", 0, c, T.h2)
    for c in CH:
        done(te, "s1", c)
        mm("sa", 1, c, u(2), T.h2, True, False)
    te.wait_ge(S.aw, n)
    te.wait_ge(S.ae, 2 * n)
    for c in CH:
        mm("sg", 0, c, T.wq[:, 0:128], T.ea, True, False)
        mm("sg", 0, c, T.wq[:, 128:256], T.eb, False, True)
        relu("sg", 0, c, T.k2)
    for c in CH:
        done(te, "sg", c)
        mm("sb", 0, c, T.wq[:, 256:384], T.k2, True, False)
    te.wait_ge(S.aqc, n)
    for c in CH:
        mm("sb", 0, c, T.wq[:, 384:512], T.qc, False, True)
        relu("sb", 0, c, T.gm)
    te.wait_ge(S.aqa, n)
    for c in CH:
        mm("sa", 1, c, v(2), T.qa, False, True)
        relu("sa", 1, c, T.h3)
    te.wait_ge(S.sw3, 16)
    for c in CH:
        done(te, "sb", c)
        mm("sc", 0, c, v(3), T.gm, True, False)
        done(te, "sa", c)
        mm("sc", 0, c, u(3), T.h3, False, True)
        relu("sc", 0, c, T.h4)

    per = NCH // NST
    for k in range(NST):
        q = g.sync if k == NST - 1 else g.scalar
        all_done(q, "sc", list(range(k * per, (k + 1) * per)))
        piece = slice(k * per * CW, (k + 1) * per * CW)
        q.dma_start(out=T.y[:, piece], in_=T.h4[:, piece]).then_inc(S["sy%d" % k], 16)
        q.wait_ge(S["sy%d" % k], 16)
    g.wait_ge(S.sent, count["sent"])
